import numpy as np
import ml_dtypes


def mxq(x, axis, fmt="e4m3"):
    dtype, down = {"e4m3": (ml_dtypes.float8_e4m3fn, 7), "e5m2": (ml_dtypes.float8_e5m2, 14)}[fmt]
    v = np.moveaxis(np.asarray(x, np.float32).astype(ml_dtypes.bfloat16).astype(np.float64), axis, -1)
    blocks = v.reshape(v.shape[:-1] + (-1, 32))
    amax = np.abs(blocks).max(-1, keepdims=True)
    byte = np.maximum(np.where(amax > 0, np.frexp(amax)[1] - 1 + 127, 0) - down, 1)
    scale = np.exp2(byte - 127.0)
    codes = (blocks / scale).astype(np.float32).astype(dtype).astype(np.float64)
    return np.moveaxis((codes * scale).reshape(v.shape), -1, axis)


WIDE = False


def mx_kscale(k):
    if not WIDE:
        return np.ones(k)
    levels = np.array([10, -10, 5, -5, 0])
    if k % 512:
        return np.exp2(np.random.permutation(np.resize(levels, k // 32))).repeat(32)
    a = np.empty((k // 512, 16))
    for p in range(k // 512):
        a[p, :8] = np.random.permutation(np.resize(levels, 8))
        for g in range(8):
            far = levels[np.abs(levels - a[p, g]) >= 10]
            a[p, g + 8] = far[np.random.randint(len(far))]
    return np.exp2(a.ravel()).repeat(32)


def f64(x):
    return np.asarray(x).astype(np.float64)


def striped8(idx):
    return np.asarray(idx).reshape(8, -1, 16).transpose(0, 2, 1).reshape(128, -1).astype(np.uint16)


def unstriped8(offs):
    return offs.reshape(8, 16, -1).transpose(0, 2, 1).reshape(8, -1).astype(np.int64)


def pick8(x, idx, run):
    r = np.arange(len(x))
    return x[r[:, None], idx[r % (8 * run) // run]]


E2M1 = np.array([0.0, 0.5, 1.0, 1.5, 2.0, 3.0, 4.0, 6.0, -0.0, -0.5, -1.0, -1.5, -2.0, -3.0, -4.0, -6.0])


def pack_weight(w, fmt):
    k, n = w.shape
    w = f64(np.asarray(w, np.float32).astype(ml_dtypes.bfloat16)).reshape(k // 32, 32, n)
    amax = np.abs(w).max(1)
    if fmt == "e4m3":
        byte = np.frexp(amax)[1] - 1 + 127 - 7
    else:
        mant, ex = np.frexp(amax / 6.0)
        byte = np.where(mant > 0.5, ex, ex - 1) + 127
    byte = np.clip(np.where(amax > 0, byte, 1), 1, 254)
    scaled = (w * np.exp2(127.0 - byte)[:, None, :]).reshape(k, n).astype(np.float32)
    by_word = np.ascontiguousarray(scaled.reshape(k // 512, 128, 4, n).transpose(0, 1, 3, 2))
    if fmt == "e4m3":
        words = by_word.astype(ml_dtypes.float8_e4m3fn).view(np.uint8)
    else:
        c = by_word.astype(ml_dtypes.float4_e2m1fn).view(np.uint8) & 0xF
        words = (c[..., 0::2] | (c[..., 1::2] << 4)).reshape(k // 512, 128, 2 * n)
    return np.ascontiguousarray(words), np.ascontiguousarray(byte.astype(np.uint8).reshape(k // 512, 16, n))


def unpack_weight(words, scales, fmt):
    g, _, n = scales.shape
    words = np.ascontiguousarray(words).reshape(g, 128, n, -1)
    if fmt == "e4m3":
        vals = words.view(ml_dtypes.float8_e4m3fn).astype(np.float64)
    else:
        nib = np.empty((g, 128, n, 4), np.uint8)
        nib[..., 0::2] = words & 0xF
        nib[..., 1::2] = words >> 4
        vals = E2M1[nib]
    vals = vals * np.repeat(np.exp2(scales.astype(np.float64) - 127.0), 8, axis=1)[..., None]
    return vals.transpose(0, 1, 3, 2).reshape(g * 512, n)


D, K, T, U, I, Q = 512, 512, 1024, 1024, 512, 128


def setup_inputs():
    n = np.random.standard_normal
    idx = np.stack([np.random.permutation(T)[:I] for _ in range(8)])
    idx2 = np.stack([np.random.permutation(U)[:I] for _ in range(8)])
    idx3 = np.stack([np.random.permutation(U)[:I] for _ in range(8)])
    fd = mx_kscale(D)
    fk = mx_kscale(K)
    wqp = pack_weight(n((D, K)) * 1.0 / np.sqrt(D) * fd[:, None] * fk, "e4m3")
    keysp = pack_weight(n((K, T)) * 1.0 / np.sqrt(K) / fk[:, None], "e4m3")
    notesp = pack_weight(n((D, U)) * 1.0 / np.sqrt(D) * fd[:, None], "e2m1")
    return {
        "states": (n((D, Q)) * 0.95 / fd[:, None]).astype(np.float32),
        "wq_words": wqp[0],
        "wq_scales": wqp[1],
        "keys_words": keysp[0],
        "keys_scales": keysp[1],
        "notes_words": notesp[0],
        "notes_scales": notesp[1],
        "offs": striped8(idx),
        "offs2": striped8(idx2),
        "offs3": striped8(idx3),
    }


def reference(states, wq_words, wq_scales, keys_words, keys_scales, notes_words, notes_scales, offs, offs2, offs3):
    idx = unstriped8(offs)
    idx2 = unstriped8(offs2)
    idx3 = unstriped8(offs3)
    wqu = unpack_weight(wq_words, wq_scales, "e4m3")
    keysu = unpack_weight(keys_words, keys_scales, "e4m3")
    notesu = unpack_weight(notes_words, notes_scales, "e2m1")
    statesq = mxq(f64(states), 0, "e4m3")
    qv = wqu.T @ statesq
    qvq = mxq(qv, 0, "e4m3")
    a = qvq.T @ keysu
    b = statesq.T @ notesu
    w = pick8(a, idx, 16) * 1.5
    w1 = np.pad(w, ((0, 0), (1, 0)))[:, :I]
    r = w - w1
    f1 = np.zeros((Q, U))
    f1[np.arange(Q)[:, None], idx2[np.arange(Q) % 128 // 16]] = r
    cc = b + f1
    y = pick8(cc, idx3, 16)
    return y

@@ -1,0 +1,175 @@
+from contextlib import ExitStack
+
+import concourse.mybir as mybir
+
+D, K, T, U, I, Q = 512, 512, 1024, 1024, 512, 128
+FLOPS = 2 * D * K * Q + 2 * K * T * Q + 2 * D * U * Q
+
+F32 = mybir.dt.float32
+BF16 = mybir.dt.bfloat16
+I32 = mybir.dt.int32
+U32 = mybir.dt.uint32
+U16 = mybir.dt.uint16
+U8 = mybir.dt.uint8
+FP8X4 = mybir.dt.float8_e4m3fn_x4
+FP4X4 = mybir.dt.float4_e2m1fn_x4
+COPY = mybir.ActivationFunctionType.Copy
+ADD = mybir.AluOpType.add
+MULT = mybir.AluOpType.mult
+
+P = 128
+PACK = 4
+HALF = I // 2
+LEAD = 8
+A_TILE = 256
+B_TILE = 512
+
+
+def load_scale_rows(queues, plane, rows):
+    for quad in range(4):
+        queues[quad].dma_start(
+            out=plane[32 * quad : 32 * quad + 4, :].bitcast(I32),
+            in_=rows[0, 4 * quad : 4 * quad + 4, :].bitcast(I32),
+        )
+
+
+def tile_attend_stepsbetween_madeside_kernel(
+    tc, states, wq_words, wq_scales, keys_words, keys_scales, notes_words, notes_scales, offs, offs2, offs3, out
+):
+    nc = tc.nc
+    with ExitStack() as ctx:
+        keep = ctx.enter_context(tc.tile_pool(name="keep", bufs=1))
+        psum = ctx.enter_context(tc.psum_pool(name="psum", bufs=1))
+
+        idx = keep.tile([P, I // 16], U16, name="idx")
+        idx2 = keep.tile([P, I // 16], U16, name="idx2")
+        idx3 = keep.tile([P, I // 16], U16, name="idx3")
+
+        wq_plane_raw = keep.tile([P, K], U8, align_bytes=64)
+        keys_plane = keep.tile([P, T], U8, align_bytes=64)
+        notes_plane = keep.tile([P, U], U8, align_bytes=64)
+        f1 = keep.tile([P, U], F32, align_bytes=64)
+        zero = keep.tile([P, 1], F32)
+        nc.vector.memset(wq_plane_raw[:].bitcast(I32), 0)
+        nc.vector.memset(keys_plane[:].bitcast(I32), 0)
+        nc.vector.memset(notes_plane[:].bitcast(I32), 0)
+        nc.vector.memset(zero[:], 0.0)
+        nc.vector.memset(f1[:], 0.0)
+
+        states_raw = keep.tile([P, PACK, Q], F32, align_bytes=64)
+        wq_raw = keep.tile([P, K], U32, align_bytes=64)
+        keys_codes = keep.tile([P, T], U32, align_bytes=64)
+        notes_codes = keep.tile([P, 2 * U], U8, align_bytes=64)
+        nc.sync.dma_start(out=states_raw[:], in_=states.rearrange("(p j) q -> p j q", j=PACK))
+        nc.sync.dma_start(out=wq_raw[:].bitcast(I32), in_=wq_words[0].rearrange("p n t -> p (n t)").bitcast(I32))
+        load_scale_rows([nc.scalar, nc.scalar, nc.sync, nc.sync], wq_plane_raw, wq_scales)
+        nc.sync.dma_start(out=keys_codes[:].bitcast(I32), in_=keys_words[0].rearrange("p n t -> p (n t)").bitcast(I32))
+        nc.sync.dma_start(out=notes_codes[:].bitcast(I32), in_=notes_words[0].bitcast(I32))
+        load_scale_rows([nc.sync] * 4, keys_plane, keys_scales)
+        nc.sync.dma_start(idx[:], offs)
+        load_scale_rows([nc.sync] * 4, notes_plane, notes_scales)
+        nc.sync.dma_start(idx2[:], offs2)
+        nc.sync.dma_start(idx3[:], offs3)
+
+        neg_w = keep.tile([P, LEAD + I], F32, align_bytes=64)
+        nc.scalar.activation(neg_w[:, LEAD - 1 : LEAD], zero[:], COPY)
+
+        states_bf = keep.tile([P, Q, PACK], BF16, align_bytes=64)
+        nc.vector.tensor_copy(
+            out=states_bf[:].rearrange("p (c i) j -> p c j i", i=4),
+            in_=states_raw[:].rearrange("p j (c i) -> p c j i", i=4),
+        )
+        wq_plane = keep.tile([P, K], U8, align_bytes=64)
+        nc.vector.tensor_copy(
+            out=wq_plane[:].rearrange("p (t h l) -> p h t l", t=PACK, l=16),
+            in_=wq_plane_raw[:].rearrange("p (h l t) -> p h t l", t=PACK, l=16),
+        )
+        wq_codes = keep.tile([P, K], U32, align_bytes=64)
+        nc.scalar.copy(
+            out=wq_codes[:].rearrange("p (t h l) -> p h t l", t=PACK, l=4),
+            in_=wq_raw[:].rearrange("p (h l t) -> p h t l", t=PACK, l=4),
+        )
+        states_codes = keep.tile([P, Q], U32, align_bytes=64)
+        states_plane = keep.tile([P, Q], U8, align_bytes=64)
+        nc.vector.quantize_mx(
+            out=states_codes[:].bitcast(FP8X4), scales=states_plane[:], in_=states_bf[:].rearrange("p q j -> p (q j)")
+        )
+
+        qv_bank = psum.tile([P, PACK, Q], F32, name="qv_bank")
+        for t in range(PACK):
+            cols = slice(t * P, (t + 1) * P)
+            nc.tensor.matmul_mx(
+                out=qv_bank[:, t, :],
+                lhsT=wq_codes[:, cols].bitcast(FP8X4),
+                lhsT_scale=wq_plane[:, cols],
+                rhs=states_codes[:].bitcast(FP8X4),
+                rhs_scale=states_plane[:],
+                start=True,
+                stop=True,
+            )
+        qv_bf = keep.tile([P, Q, PACK], BF16, align_bytes=64)
+        nc.scalar.copy(out=qv_bf[:], in_=qv_bank[:].rearrange("p t q -> p q t"))
+        qv_codes = keep.tile([P, Q], U32, align_bytes=64)
+        qv_plane = keep.tile([P, Q], U8, align_bytes=64)
+        nc.vector.quantize_mx(
+            out=qv_codes[:].bitcast(FP8X4), scales=qv_plane[:], in_=qv_bf[:].rearrange("p q t -> p (q t)")
+        )
+
+        a = keep.tile([P, T], F32, align_bytes=64)
+        for n in range(T // A_TILE):
+            cols = slice(n * A_TILE, (n + 1) * A_TILE)
+            a_bank = psum.tile([P, A_TILE], F32, name="a_bank%d" % n)
+            nc.tensor.matmul_mx(
+                out=a_bank[:],
+                lhsT=qv_codes[:].bitcast(FP8X4),
+                lhsT_scale=qv_plane[:],
+                rhs=keys_codes[:, cols].bitcast(FP8X4),
+                rhs_scale=keys_plane[:, cols],
+                start=True,
+                stop=True,
+            )
+            if n % 2 == 0:
+                nc.vector.tensor_copy(out=a[:, cols], in_=a_bank[:])
+            else:
+                nc.scalar.copy(out=a[:, cols], in_=a_bank[:])
+
+        b_banks = []
+        for n in range(U // B_TILE):
+            b_bank = psum.tile([P, B_TILE], F32, name="b_bank%d" % n)
+            nc.tensor.matmul_mx(
+                out=b_bank[:],
+                lhsT=states_codes[:].bitcast(FP8X4),
+                lhsT_scale=states_plane[:],
+                rhs=notes_codes[:, 2 * n * B_TILE : 2 * (n + 1) * B_TILE].bitcast(FP4X4),
+                rhs_scale=notes_plane[:, n * B_TILE : (n + 1) * B_TILE],
+                start=True,
+                stop=True,
+            )
+            b_banks.append(b_bank)
+
+        cols_half = HALF // 16
+        w_lo = keep.tile([P, HALF], F32, align_bytes=64)
+        w_hi = keep.tile([P, HALF], F32, align_bytes=64)
+        nc.vector.tensor_scalar(w_lo[:], a[:].indirect(idx[:, 0:cols_half]), 1.5, 0.0, MULT, ADD)
+        nc.scalar.activation(neg_w[:, LEAD : LEAD + HALF], a[:].indirect(idx[:, 0:cols_half]), COPY, scale=-1.5)
+        nc.scalar.activation(w_hi[:], a[:].indirect(idx[:, cols_half : 2 * cols_half]), COPY, scale=1.5)
+        nc.scalar.activation(neg_w[:, LEAD + HALF : LEAD + I - 1], w_hi[:, 0 : HALF - 1], COPY, scale=-1.0)
+
+        nc.vector.tensor_tensor(
+            f1[:].indirect(idx2[:, 0:cols_half]), w_lo[:], neg_w[:, LEAD - 1 : LEAD - 1 + HALF], ADD
+        )
+        nc.vector.tensor_tensor(
+            f1[:].indirect(idx2[:, cols_half : 2 * cols_half]), w_hi[:], neg_w[:, LEAD - 1 + HALF : LEAD - 1 + I], ADD
+        )
+
+        cc = keep.tile([P, U], F32, align_bytes=64)
+        for n in range(U // B_TILE):
+            cols = slice(n * B_TILE, (n + 1) * B_TILE)
+            nc.vector.tensor_tensor(cc[:, cols], b_banks[n][:], f1[:, cols], ADD)
+
+        y_lo = keep.tile([P, HALF], F32, align_bytes=64)
+        y_hi = keep.tile([P, HALF], F32, align_bytes=64)
+        nc.vector.tensor_copy(y_lo[:], cc[:].indirect(idx3[:, 0:cols_half]))
+        nc.scalar.activation(y_hi[:], cc[:].indirect(idx3[:, cols_half : 2 * cols_half]), COPY)
+        nc.sync.dma_start(out=out[:, 0:HALF], in_=y_lo[:])
+        nc.scalar.dma_start(out=out[:, HALF:I], in_=y_hi[:])

@@ -21,8 +21,10 @@ P = 128
 PACK = 4
 HALF = I // 2
 LEAD = 8
-A_TILE = 256
+A_WIDTHS = (256, 256, 256, 128, 128)
 B_TILE = 512
+CAST_V = 64
+ADD_G = 256
 
 
 def load_scale_rows(queues, plane, rows):
@@ -49,35 +51,39 @@ def tile_attend_stepsbetween_madeside_kernel(
         keys_plane = keep.tile([P, T], U8, align_bytes=64)
         notes_plane = keep.tile([P, U], U8, align_bytes=64)
         f1 = keep.tile([P, U], F32, align_bytes=64)
-        zero = keep.tile([P, 1], F32)
+        neg_w = keep.tile([P, LEAD + I], F32, align_bytes=64)
         nc.vector.memset(wq_plane_raw[:].bitcast(I32), 0)
         nc.vector.memset(keys_plane[:].bitcast(I32), 0)
         nc.vector.memset(notes_plane[:].bitcast(I32), 0)
-        nc.vector.memset(zero[:], 0.0)
+        nc.vector.memset(neg_w[:, 0:LEAD], 0.0)
         nc.vector.memset(f1[:], 0.0)
 
         states_raw = keep.tile([P, PACK, Q], F32, align_bytes=64)
-        wq_raw = keep.tile([P, K], U32, align_bytes=64)
+        wq_raw = [keep.tile([P, K // 2], U32, align_bytes=64, name="wq_raw%d" % h) for h in range(2)]
         keys_codes = keep.tile([P, T], U32, align_bytes=64)
         notes_codes = keep.tile([P, 2 * U], U8, align_bytes=64)
         nc.sync.dma_start(out=states_raw[:], in_=states.rearrange("(p j) q -> p j q", j=PACK))
-        nc.sync.dma_start(out=wq_raw[:].bitcast(I32), in_=wq_words[0].rearrange("p n t -> p (n t)").bitcast(I32))
         load_scale_rows([nc.scalar, nc.scalar, nc.sync, nc.sync], wq_plane_raw, wq_scales)
+        wq_rows = wq_words[0].rearrange("p n t -> p (n t)").bitcast(I32)
+        for h in range(2):
+            nc.sync.dma_start(out=wq_raw[h][:].bitcast(I32), in_=wq_rows[:, h * (K // 2) : (h + 1) * (K // 2)])
         nc.sync.dma_start(out=keys_codes[:].bitcast(I32), in_=keys_words[0].rearrange("p n t -> p (n t)").bitcast(I32))
-        nc.sync.dma_start(out=notes_codes[:].bitcast(I32), in_=notes_words[0].bitcast(I32))
         load_scale_rows([nc.sync] * 4, keys_plane, keys_scales)
         nc.sync.dma_start(idx[:], offs)
+        nc.sync.dma_start(out=notes_codes[:].bitcast(I32), in_=notes_words[0].bitcast(I32))
         load_scale_rows([nc.sync] * 4, notes_plane, notes_scales)
         nc.sync.dma_start(idx2[:], offs2)
         nc.sync.dma_start(idx3[:], offs3)
 
-        neg_w = keep.tile([P, LEAD + I], F32, align_bytes=64)
-        nc.scalar.activation(neg_w[:, LEAD - 1 : LEAD], zero[:], COPY)
-
         states_bf = keep.tile([P, Q, PACK], BF16, align_bytes=64)
         nc.vector.tensor_copy(
-            out=states_bf[:].rearrange("p (c i) j -> p c j i", i=4),
-            in_=states_raw[:].rearrange("p j (c i) -> p c j i", i=4),
+            out=states_bf[:, 0:CAST_V, :].rearrange("p (c i) j -> p c j i", i=4),
+            in_=states_raw[:, :, 0:CAST_V].rearrange("p j (c i) -> p c j i", i=4),
+        )
+        nc.scalar.activation(
+            states_bf[:, CAST_V:Q, :].rearrange("p (c i) j -> p c j i", i=4),
+            states_raw[:, :, CAST_V:Q].rearrange("p j (c i) -> p c j i", i=4),
+            COPY,
         )
         wq_plane = keep.tile([P, K], U8, align_bytes=64)
         nc.vector.tensor_copy(
@@ -85,21 +91,23 @@ def tile_attend_stepsbetween_madeside_kernel(
             in_=wq_plane_raw[:].rearrange("p (h l t) -> p h t l", t=PACK, l=16),
         )
         wq_codes = keep.tile([P, K], U32, align_bytes=64)
-        nc.scalar.copy(
-            out=wq_codes[:].rearrange("p (t h l) -> p h t l", t=PACK, l=4),
-            in_=wq_raw[:].rearrange("p (h l t) -> p h t l", t=PACK, l=4),
-        )
+        dealt = wq_codes[:].rearrange("p (t h g l) -> p h g t l", t=PACK, h=2, l=4)
+        undealt = [wq_raw[h][:].rearrange("p (g l t) -> p g t l", t=PACK, l=4) for h in range(2)]
+        for h in range(2):
+            nc.scalar.copy(out=dealt[:, h, :, 0:2, :], in_=undealt[h][:, :, 0:2, :])
         states_codes = keep.tile([P, Q], U32, align_bytes=64)
         states_plane = keep.tile([P, Q], U8, align_bytes=64)
         nc.vector.quantize_mx(
             out=states_codes[:].bitcast(FP8X4), scales=states_plane[:], in_=states_bf[:].rearrange("p q j -> p (q j)")
         )
+        for h in range(2):
+            nc.vector.tensor_copy(out=dealt[:, h, :, 2:4, :].bitcast(I32), in_=undealt[h][:, :, 2:4, :].bitcast(I32))
 
-        qv_bank = psum.tile([P, PACK, Q], F32, name="qv_bank")
+        qv_banks = [psum.tile([P, 2, Q], F32, name="qv_bank%d" % h, tag="bank%d" % h) for h in range(2)]
         for t in range(PACK):
             cols = slice(t * P, (t + 1) * P)
             nc.tensor.matmul_mx(
-                out=qv_bank[:, t, :],
+                out=qv_banks[t // 2][:, t % 2, :],
                 lhsT=wq_codes[:, cols].bitcast(FP8X4),
                 lhsT_scale=wq_plane[:, cols],
                 rhs=states_codes[:].bitcast(FP8X4),
@@ -108,7 +116,8 @@ def tile_attend_stepsbetween_madeside_kernel(
                 stop=True,
             )
         qv_bf = keep.tile([P, Q, PACK], BF16, align_bytes=64)
-        nc.scalar.copy(out=qv_bf[:], in_=qv_bank[:].rearrange("p t q -> p q t"))
+        nc.vector.tensor_copy(out=qv_bf[:, :, 0:2], in_=qv_banks[0][:].rearrange("p t q -> p q t"))
+        nc.scalar.copy(out=qv_bf[:, :, 2:4], in_=qv_banks[1][:].rearrange("p t q -> p q t"))
         qv_codes = keep.tile([P, Q], U32, align_bytes=64)
         qv_plane = keep.tile([P, Q], U8, align_bytes=64)
         nc.vector.quantize_mx(
@@ -116,9 +125,10 @@ def tile_attend_stepsbetween_madeside_kernel(
         )
 
         a = keep.tile([P, T], F32, align_bytes=64)
-        for n in range(T // A_TILE):
-            cols = slice(n * A_TILE, (n + 1) * A_TILE)
-            a_bank = psum.tile([P, A_TILE], F32, name="a_bank%d" % n)
+        for n, width in enumerate(A_WIDTHS):
+            first = sum(A_WIDTHS[:n])
+            cols = slice(first, first + width)
+            a_bank = psum.tile([P, width], F32, name="a_bank%d" % n, tag="bank%d" % ((n + 2) % 6))
             nc.tensor.matmul_mx(
                 out=a_bank[:],
                 lhsT=qv_codes[:].bitcast(FP8X4),
@@ -154,6 +164,8 @@ def tile_attend_stepsbetween_madeside_kernel(
         nc.scalar.activation(neg_w[:, LEAD : LEAD + HALF], a[:].indirect(idx[:, 0:cols_half]), COPY, scale=-1.5)
         nc.scalar.activation(w_hi[:], a[:].indirect(idx[:, cols_half : 2 * cols_half]), COPY, scale=1.5)
         nc.scalar.activation(neg_w[:, LEAD + HALF : LEAD + I - 1], w_hi[:, 0 : HALF - 1], COPY, scale=-1.0)
+        b_tail = keep.tile([P, ADD_G], F32, align_bytes=64)
+        nc.scalar.copy(out=b_tail[:], in_=b_banks[1][:, B_TILE - ADD_G : B_TILE])
 
         nc.vector.tensor_tensor(
             f1[:].indirect(idx2[:, 0:cols_half]), w_lo[:], neg_w[:, LEAD - 1 : LEAD - 1 + HALF], ADD
@@ -163,9 +175,10 @@ def tile_attend_stepsbetween_madeside_kernel(
         )
 
         cc = keep.tile([P, U], F32, align_bytes=64)
-        for n in range(U // B_TILE):
-            cols = slice(n * B_TILE, (n + 1) * B_TILE)
-            nc.vector.tensor_tensor(cc[:, cols], b_banks[n][:], f1[:, cols], ADD)
+        split = U - ADD_G
+        nc.gpsimd.tensor_tensor(cc[:, split:U], b_tail[:], f1[:, split:U], ADD)
+        nc.vector.tensor_tensor(cc[:, 0:B_TILE], b_banks[0][:], f1[:, 0:B_TILE], ADD)
+        nc.vector.tensor_tensor(cc[:, B_TILE:split], b_banks[1][:, 0 : split - B_TILE], f1[:, B_TILE:split], ADD)
 
         y_lo = keep.tile([P, HALF], F32, align_bytes=64)
         y_hi = keep.tile([P, HALF], F32, align_bytes=64)

@@ -23,7 +23,6 @@ HALF = I // 2
 LEAD = 8
 A_WIDTHS = (256, 256, 256, 128, 128)
 B_TILE = 512
-CAST_V = 64
 ADD_G = 256
 
 
@@ -55,18 +54,17 @@ def tile_attend_stepsbetween_madeside_kernel(
         nc.vector.memset(wq_plane_raw[:].bitcast(I32), 0)
         nc.vector.memset(keys_plane[:].bitcast(I32), 0)
         nc.vector.memset(notes_plane[:].bitcast(I32), 0)
-        nc.vector.memset(neg_w[:, 0:LEAD], 0.0)
+        zero = keep.tile([P, 1], F32)
+        nc.vector.memset(zero[:], 0.0)
         nc.vector.memset(f1[:], 0.0)
 
         states_raw = keep.tile([P, PACK, Q], F32, align_bytes=64)
-        wq_raw = [keep.tile([P, K // 2], U32, align_bytes=64, name="wq_raw%d" % h) for h in range(2)]
+        wq_raw = keep.tile([P, K], U32, align_bytes=64)
         keys_codes = keep.tile([P, T], U32, align_bytes=64)
         notes_codes = keep.tile([P, 2 * U], U8, align_bytes=64)
         nc.sync.dma_start(out=states_raw[:], in_=states.rearrange("(p j) q -> p j q", j=PACK))
+        nc.sync.dma_start(out=wq_raw[:].bitcast(I32), in_=wq_words[0].rearrange("p n t -> p (n t)").bitcast(I32))
         load_scale_rows([nc.scalar, nc.scalar, nc.sync, nc.sync], wq_plane_raw, wq_scales)
-        wq_rows = wq_words[0].rearrange("p n t -> p (n t)").bitcast(I32)
-        for h in range(2):
-            nc.sync.dma_start(out=wq_raw[h][:].bitcast(I32), in_=wq_rows[:, h * (K // 2) : (h + 1) * (K // 2)])
         nc.sync.dma_start(out=keys_codes[:].bitcast(I32), in_=keys_words[0].rearrange("p n t -> p (n t)").bitcast(I32))
         load_scale_rows([nc.sync] * 4, keys_plane, keys_scales)
         nc.sync.dma_start(idx[:], offs)
@@ -75,33 +73,28 @@ def tile_attend_stepsbetween_madeside_kernel(
         nc.sync.dma_start(idx2[:], offs2)
         nc.sync.dma_start(idx3[:], offs3)
 
+        nc.scalar.activation(neg_w[:, LEAD - 1 : LEAD], zero[:], COPY)
+
         states_bf = keep.tile([P, Q, PACK], BF16, align_bytes=64)
         nc.vector.tensor_copy(
-            out=states_bf[:, 0:CAST_V, :].rearrange("p (c i) j -> p c j i", i=4),
-            in_=states_raw[:, :, 0:CAST_V].rearrange("p j (c i) -> p c j i", i=4),
+            out=states_bf[:].rearrange("p (c i) j -> p c j i", i=4),
+            in_=states_raw[:].rearrange("p j (c i) -> p c j i", i=4),
         )
-        nc.scalar.activation(
-            states_bf[:, CAST_V:Q, :].rearrange("p (c i) j -> p c j i", i=4),
-            states_raw[:, :, CAST_V:Q].rearrange("p j (c i) -> p c j i", i=4),
-            COPY,
-        )
-        wq_plane = keep.tile([P, K], U8, align_bytes=64)
-        nc.vector.tensor_copy(
-            out=wq_plane[:].rearrange("p (t h l) -> p h t l", t=PACK, l=16),
-            in_=wq_plane_raw[:].rearrange("p (h l t) -> p h t l", t=PACK, l=16),
-        )
-        wq_codes = keep.tile([P, K], U32, align_bytes=64)
-        dealt = wq_codes[:].rearrange("p (t h g l) -> p h g t l", t=PACK, h=2, l=4)
-        undealt = [wq_raw[h][:].rearrange("p (g l t) -> p g t l", t=PACK, l=4) for h in range(2)]
-        for h in range(2):
-            nc.scalar.copy(out=dealt[:, h, :, 0:2, :], in_=undealt[h][:, :, 0:2, :])
         states_codes = keep.tile([P, Q], U32, align_bytes=64)
         states_plane = keep.tile([P, Q], U8, align_bytes=64)
         nc.vector.quantize_mx(
             out=states_codes[:].bitcast(FP8X4), scales=states_plane[:], in_=states_bf[:].rearrange("p q j -> p (q j)")
         )
-        for h in range(2):
-            nc.vector.tensor_copy(out=dealt[:, h, :, 2:4, :].bitcast(I32), in_=undealt[h][:, :, 2:4, :].bitcast(I32))
+
+        wq_plane = keep.tile([P, K], U8, align_bytes=64)
+        wq_codes = keep.tile([P, K], U32, align_bytes=64)
+        plane_dealt = wq_plane[:].rearrange("p (t g l) -> p g t l", t=PACK, l=16)
+        plane_undealt = wq_plane_raw[:].rearrange("p (g l t) -> p g t l", t=PACK, l=16)
+        codes_dealt = wq_codes[:].rearrange("p (t g l) -> p g t l", t=PACK, l=4)
+        codes_undealt = wq_raw[:].rearrange("p (g l t) -> p g t l", t=PACK, l=4)
+        for pair in (slice(0, 2), slice(2, 4)):
+            nc.vector.tensor_copy(out=plane_dealt[:, :, pair, :], in_=plane_undealt[:, :, pair, :])
+            nc.scalar.copy(out=codes_dealt[:, :, pair, :], in_=codes_undealt[:, :, pair, :])
 
         qv_banks = [psum.tile([P, 2, Q], F32, name="qv_bank%d" % h, tag="bank%d" % h) for h in range(2)]
         for t in range(PACK):

from contextlib import ExitStack

import concourse.mybir as mybir

D, K, T, U, I, Q = 512, 512, 1024, 1024, 512, 128
FLOPS = 2 * D * K * Q + 2 * K * T * Q + 2 * D * U * Q

F32 = mybir.dt.float32
BF16 = mybir.dt.bfloat16
I32 = mybir.dt.int32
U32 = mybir.dt.uint32
U16 = mybir.dt.uint16
U8 = mybir.dt.uint8
FP8X4 = mybir.dt.float8_e4m3fn_x4
FP4X4 = mybir.dt.float4_e2m1fn_x4
COPY = mybir.ActivationFunctionType.Copy
ADD = mybir.AluOpType.add
MULT = mybir.AluOpType.mult

P = 128
PACK = 4
HALF = I // 2
LEAD = 8
A_WIDTHS = (256, 256, 256, 128, 128)
B_TILE = 512
ADD_G = 256


def load_scale_rows(queues, plane, rows):
    for quad in range(4):
        queues[quad].dma_start(
            out=plane[32 * quad : 32 * quad + 4, :].bitcast(I32),
            in_=rows[0, 4 * quad : 4 * quad + 4, :].bitcast(I32),
        )


def tile_attend_stepsbetween_madeside_kernel(
    tc, states, wq_words, wq_scales, keys_words, keys_scales, notes_words, notes_scales, offs, offs2, offs3, out
):
    nc = tc.nc
    with ExitStack() as ctx:
        keep = ctx.enter_context(tc.tile_pool(name="keep", bufs=1))
        psum = ctx.enter_context(tc.psum_pool(name="psum", bufs=1))

        idx = keep.tile([P, I // 16], U16, name="idx")
        idx2 = keep.tile([P, I // 16], U16, name="idx2")
        idx3 = keep.tile([P, I // 16], U16, name="idx3")

        wq_plane_raw = keep.tile([P, K], U8, align_bytes=64)
        keys_plane = keep.tile([P, T], U8, align_bytes=64)
        notes_plane = keep.tile([P, U], U8, align_bytes=64)
        f1 = keep.tile([P, U], F32, align_bytes=64)
        neg_w = keep.tile([P, LEAD + I], F32, align_bytes=64)
        nc.vector.memset(wq_plane_raw[:].bitcast(I32), 0)
        nc.vector.memset(keys_plane[:].bitcast(I32), 0)
        nc.vector.memset(notes_plane[:].bitcast(I32), 0)
        zero = keep.tile([P, 1], F32)
        nc.vector.memset(zero[:], 0.0)
        nc.vector.memset(f1[:], 0.0)

        states_raw = keep.tile([P, PACK, Q], F32, align_bytes=64)
        wq_raw = keep.tile([P, K], U32, align_bytes=64)
        keys_codes = keep.tile([P, T], U32, align_bytes=64)
        notes_codes = keep.tile([P, 2 * U], U8, align_bytes=64)
        nc.sync.dma_start(out=states_raw[:], in_=states.rearrange("(p j) q -> p j q", j=PACK))
        nc.sync.dma_start(out=wq_raw[:].bitcast(I32), in_=wq_words[0].rearrange("p n t -> p (n t)").bitcast(I32))
        load_scale_rows([nc.scalar, nc.scalar, nc.sync, nc.sync], wq_plane_raw, wq_scales)
        nc.sync.dma_start(out=keys_codes[:].bitcast(I32), in_=keys_words[0].rearrange("p n t -> p (n t)").bitcast(I32))
        load_scale_rows([nc.sync] * 4, keys_plane, keys_scales)
        nc.sync.dma_start(idx[:], offs)
        nc.sync.dma_start(out=notes_codes[:].bitcast(I32), in_=notes_words[0].bitcast(I32))
        load_scale_rows([nc.sync] * 4, notes_plane, notes_scales)
        nc.sync.dma_start(idx2[:], offs2)
        nc.sync.dma_start(idx3[:], offs3)

        nc.scalar.activation(neg_w[:, LEAD - 1 : LEAD], zero[:], COPY)

        states_bf = keep.tile([P, Q, PACK], BF16, align_bytes=64)
        nc.vector.tensor_copy(
            out=states_bf[:].rearrange("p (c i) j -> p c j i", i=4),
            in_=states_raw[:].rearrange("p j (c i) -> p c j i", i=4),
        )
        states_codes = keep.tile([P, Q], U32, align_bytes=64)
        states_plane = keep.tile([P, Q], U8, align_bytes=64)
        nc.vector.quantize_mx(
            out=states_codes[:].bitcast(FP8X4), scales=states_plane[:], in_=states_bf[:].rearrange("p q j -> p (q j)")
        )

        wq_plane = keep.tile([P, K], U8, align_bytes=64)
        wq_codes = keep.tile([P, K], U32, align_bytes=64)
        plane_dealt = wq_plane[:].rearrange("p (t g l) -> p g t l", t=PACK, l=16)
        plane_undealt = wq_plane_raw[:].rearrange("p (g l t) -> p g t l", t=PACK, l=16)
        codes_dealt = wq_codes[:].rearrange("p (t g l) -> p g t l", t=PACK, l=4)
        codes_undealt = wq_raw[:].rearrange("p (g l t) -> p g t l", t=PACK, l=4)
        for pair in (slice(0, 2), slice(2, 4)):
            nc.vector.tensor_copy(out=plane_dealt[:, :, pair, :], in_=plane_undealt[:, :, pair, :])
            nc.scalar.copy(out=codes_dealt[:, :, pair, :], in_=codes_undealt[:, :, pair, :])

        qv_banks = [psum.tile([P, 2, Q], F32, name="qv_bank%d" % h, tag="bank%d" % h) for h in range(2)]
        for t in range(PACK):
            cols = slice(t * P, (t + 1) * P)
            nc.tensor.matmul_mx(
                out=qv_banks[t // 2][:, t % 2, :],
                lhsT=wq_codes[:, cols].bitcast(FP8X4),
                lhsT_scale=wq_plane[:, cols],
                rhs=states_codes[:].bitcast(FP8X4),
                rhs_scale=states_plane[:],
                start=True,
                stop=True,
            )
        qv_bf = keep.tile([P, Q, PACK], BF16, align_bytes=64)
        nc.vector.tensor_copy(out=qv_bf[:, :, 0:2], in_=qv_banks[0][:].rearrange("p t q -> p q t"))
        nc.scalar.copy(out=qv_bf[:, :, 2:4], in_=qv_banks[1][:].rearrange("p t q -> p q t"))
        qv_codes = keep.tile([P, Q], U32, align_bytes=64)
        qv_plane = keep.tile([P, Q], U8, align_bytes=64)
        nc.vector.quantize_mx(
            out=qv_codes[:].bitcast(FP8X4), scales=qv_plane[:], in_=qv_bf[:].rearrange("p q t -> p (q t)")
        )

        a = keep.tile([P, T], F32, align_bytes=64)
        for n, width in enumerate(A_WIDTHS):
            first = sum(A_WIDTHS[:n])
            cols = slice(first, first + width)
            a_bank = psum.tile([P, width], F32, name="a_bank%d" % n, tag="bank%d" % ((n + 2) % 6))
            nc.tensor.matmul_mx(
                out=a_bank[:],
                lhsT=qv_codes[:].bitcast(FP8X4),
                lhsT_scale=qv_plane[:],
                rhs=keys_codes[:, cols].bitcast(FP8X4),
                rhs_scale=keys_plane[:, cols],
                start=True,
                stop=True,
            )
            if n % 2 == 0:
                nc.vector.tensor_copy(out=a[:, cols], in_=a_bank[:])
            else:
                nc.scalar.copy(out=a[:, cols], in_=a_bank[:])

        b_banks = []
        for n in range(U // B_TILE):
            b_bank = psum.tile([P, B_TILE], F32, name="b_bank%d" % n)
            nc.tensor.matmul_mx(
                out=b_bank[:],
                lhsT=states_codes[:].bitcast(FP8X4),
                lhsT_scale=states_plane[:],
                rhs=notes_codes[:, 2 * n * B_TILE : 2 * (n + 1) * B_TILE].bitcast(FP4X4),
                rhs_scale=notes_plane[:, n * B_TILE : (n + 1) * B_TILE],
                start=True,
                stop=True,
            )
            b_banks.append(b_bank)

        cols_half = HALF // 16
        w_lo = keep.tile([P, HALF], F32, align_bytes=64)
        w_hi = keep.tile([P, HALF], F32, align_bytes=64)
        nc.vector.tensor_scalar(w_lo[:], a[:].indirect(idx[:, 0:cols_half]), 1.5, 0.0, MULT, ADD)
        nc.scalar.activation(neg_w[:, LEAD : LEAD + HALF], a[:].indirect(idx[:, 0:cols_half]), COPY, scale=-1.5)
        nc.scalar.activation(w_hi[:], a[:].indirect(idx[:, cols_half : 2 * cols_half]), COPY, scale=1.5)
        nc.scalar.activation(neg_w[:, LEAD + HALF : LEAD + I - 1], w_hi[:, 0 : HALF - 1], COPY, scale=-1.0)
        b_tail = keep.tile([P, ADD_G], F32, align_bytes=64)
        nc.scalar.copy(out=b_tail[:], in_=b_banks[1][:, B_TILE - ADD_G : B_TILE])

        nc.vector.tensor_tensor(
            f1[:].indirect(idx2[:, 0:cols_half]), w_lo[:], neg_w[:, LEAD - 1 : LEAD - 1 + HALF], ADD
        )
        nc.vector.tensor_tensor(
            f1[:].indirect(idx2[:, cols_half : 2 * cols_half]), w_hi[:], neg_w[:, LEAD - 1 + HALF : LEAD - 1 + I], ADD
        )

        cc = keep.tile([P, U], F32, align_bytes=64)
        split = U - ADD_G
        nc.gpsimd.tensor_tensor(cc[:, split:U], b_tail[:], f1[:, split:U], ADD)
        nc.vector.tensor_tensor(cc[:, 0:B_TILE], b_banks[0][:], f1[:, 0:B_TILE], ADD)
        nc.vector.tensor_tensor(cc[:, B_TILE:split], b_banks[1][:, 0 : split - B_TILE], f1[:, B_TILE:split], ADD)

        y_lo = keep.tile([P, HALF], F32, align_bytes=64)
        y_hi = keep.tile([P, HALF], F32, align_bytes=64)
        nc.vector.tensor_copy(y_lo[:], cc[:].indirect(idx3[:, 0:cols_half]))
        nc.scalar.activation(y_hi[:], cc[:].indirect(idx3[:, cols_half : 2 * cols_half]), COPY)
        nc.sync.dma_start(out=out[:, 0:HALF], in_=y_lo[:])
        nc.scalar.dma_start(out=out[:, HALF:I], in_=y_hi[:])
